import numpy as np
import ml_dtypes


def mxq(x, axis, fmt="e4m3"):
    dtype, down = {"e4m3": (ml_dtypes.float8_e4m3fn, 7), "e5m2": (ml_dtypes.float8_e5m2, 14)}[fmt]
    v = np.moveaxis(np.asarray(x, np.float32).astype(ml_dtypes.bfloat16).astype(np.float64), axis, -1)
    blocks = v.reshape(v.shape[:-1] + (-1, 32))
    amax = np.abs(blocks).max(-1, keepdims=True)
    byte = np.maximum(np.where(amax > 0, np.frexp(amax)[1] - 1 + 127, 0) - down, 1)
    scale = np.exp2(byte - 127.0)
    codes = (blocks / scale).astype(np.float32).astype(dtype).astype(np.float64)
    return np.moveaxis((codes * scale).reshape(v.shape), -1, axis)


WIDE = False


def mx_kscale(k):
    if not WIDE:
        return np.ones(k)
    levels = np.array([10, -10, 5, -5, 0])
    if k % 512:
        return np.exp2(np.random.permutation(np.resize(levels, k // 32))).repeat(32)
    a = np.empty((k // 512, 16))
    for p in range(k // 512):
        a[p, :8] = np.random.permutation(np.resize(levels, 8))
        for g in range(8):
            far = levels[np.abs(levels - a[p, g]) >= 10]
            a[p, g + 8] = far[np.random.randint(len(far))]
    return np.exp2(a.ravel()).repeat(32)


def f64(x):
    return np.asarray(x).astype(np.float64)


def striped(idx):
    return np.tile(idx.reshape(-1, 16).T, (8, 1)).astype(np.uint16)


def unstriped(offs):
    return offs[:16].T.reshape(-1).astype(np.int64)


E2M1 = np.array([0.0, 0.5, 1.0, 1.5, 2.0, 3.0, 4.0, 6.0, -0.0, -0.5, -1.0, -1.5, -2.0, -3.0, -4.0, -6.0])


def pack_weight(w, fmt):
    k, n = w.shape
    w = f64(np.asarray(w, np.float32).astype(ml_dtypes.bfloat16)).reshape(k // 32, 32, n)
    amax = np.abs(w).max(1)
    if fmt == "e4m3":
        byte = np.frexp(amax)[1] - 1 + 127 - 7
    else:
        mant, ex = np.frexp(amax / 6.0)
        byte = np.where(mant > 0.5, ex, ex - 1) + 127
    byte = np.clip(np.where(amax > 0, byte, 1), 1, 254)
    scaled = (w * np.exp2(127.0 - byte)[:, None, :]).reshape(k, n).astype(np.float32)
    by_word = np.ascontiguousarray(scaled.reshape(k // 512, 128, 4, n).transpose(0, 1, 3, 2))
    if fmt == "e4m3":
        words = by_word.astype(ml_dtypes.float8_e4m3fn).view(np.uint8)
    else:
        c = by_word.astype(ml_dtypes.float4_e2m1fn).view(np.uint8) & 0xF
        words = (c[..., 0::2] | (c[..., 1::2] << 4)).reshape(k // 512, 128, 2 * n)
    return np.ascontiguousarray(words), np.ascontiguousarray(byte.astype(np.uint8).reshape(k // 512, 16, n))


def unpack_weight(words, scales, fmt):
    g, _, n = scales.shape
    words = np.ascontiguousarray(words).reshape(g, 128, n, -1)
    if fmt == "e4m3":
        vals = words.view(ml_dtypes.float8_e4m3fn).astype(np.float64)
    else:
        nib = np.empty((g, 128, n, 4), np.uint8)
        nib[..., 0::2] = words & 0xF
        nib[..., 1::2] = words >> 4
        vals = E2M1[nib]
    vals = vals * np.repeat(np.exp2(scales.astype(np.float64) - 127.0), 8, axis=1)[..., None]
    return vals.transpose(0, 1, 3, 2).reshape(g * 512, n)


def relu(v):
    return np.maximum(v, 0.0)


K, T, E, C, H, N = 1024, 640, 2, 256, 1024, 256


def by_expert(wq, xq):
    return np.concatenate([wq[e].T @ xq[:, e * C:(e + 1) * C] for e in range(E)], axis=1)


def setup_inputs():
    n = np.random.standard_normal
    s = mx_kscale(K)[:, None]
    u = mx_kscale(H)
    w1 = [pack_weight(m, "e2m1") for m in n((E, K, H)) / np.sqrt(K) / s[None]]
    w3 = [pack_weight(m, "e2m1") for m in n((E, K, H)) / np.sqrt(K) / s[None] * u[None, None, :]]
    w2 = [pack_weight(m, "e2m1") for m in n((E, H, N)) / np.sqrt(H) / u[None, :, None]]
    return {
        "xT": (n((K, T)) * s).astype(np.float32),
        "xr": n((N, T)).astype(np.float32),
        "w1_words": np.stack([m[0] for m in w1]),
        "w1_scales": np.stack([m[1] for m in w1]),
        "w3_words": np.stack([m[0] for m in w3]),
        "w3_scales": np.stack([m[1] for m in w3]),
        "w2_words": np.stack([m[0] for m in w2]),
        "w2_scales": np.stack([m[1] for m in w2]),
        "gate": np.tile(np.random.uniform(0.2, 1.0, E * C), (N, 1)).astype(np.float32),
        "offs": striped(np.random.permutation(T)[:E * C]),
    }


def reference(xT, xr, w1_words, w1_scales, w3_words, w3_scales, w2_words, w2_scales, gate, offs):
    idx = unstriped(offs)
    w1 = np.stack([unpack_weight(w1_words[e], w1_scales[e], "e2m1") for e in range(E)])
    w3 = np.stack([unpack_weight(w3_words[e], w3_scales[e], "e2m1") for e in range(E)])
    w2 = np.stack([unpack_weight(w2_words[e], w2_scales[e], "e2m1") for e in range(E)])
    xq = mxq(f64(xT)[:, idx], 0, "e4m3")
    h = relu(by_expert(w1, xq))
    h = h * by_expert(w3, xq)
    y = by_expert(w2, mxq(h, 0, "e4m3"))
    out = f64(xr).copy()
    out[:, idx] += f64(gate) * y
    return out

@@ -1,0 +1,232 @@
+from contextlib import ExitStack
+
+import concourse.mybir as mybir
+from concourse.masks import make_identity
+
+FLOPS = 2 * 512 * (1024 * 1024 * 2 + 1024 * 256)
+
+F32 = mybir.dt.float32
+BF16 = mybir.dt.bfloat16
+U32 = mybir.dt.uint32
+I32 = mybir.dt.int32
+U16 = mybir.dt.uint16
+U8 = mybir.dt.uint8
+FP8X4 = mybir.dt.float8_e4m3fn_x4
+FP4X4 = mybir.dt.float4_e2m1fn_x4
+COPY = mybir.ActivationFunctionType.Copy
+RELU = mybir.ActivationFunctionType.Relu
+ADD = mybir.AluOpType.add
+MULT = mybir.AluOpType.mult
+
+P = 128
+K, T, E, C, H, N = 1024, 640, 2, 256, 1024, 256
+KS = K // 512
+HS = H // 512
+NB = N // P
+SLOTS = E * C
+CHUNKS = ((0, 384), (384, 640))
+CASTS = (
+    ((0, 256, "v"), (256, 384, "s"), (384, 512, "v"), (512, 640, "s")),
+    ((0, 256, "s"), (256, 384, "s"), (384, 512, "v"), (512, 640, "s")),
+)
+QUANTS = ((0, 256), (256, 384), (384, 640))
+
+
+def tile_moe_res_glu_relu_kernel(
+    tc, xT, xr, w1_words, w1_scales, w3_words, w3_scales, w2_words, w2_scales, gate, offs, out
+):
+    nc = tc.nc
+    with ExitStack() as ctx:
+        keep = ctx.enter_context(tc.tile_pool(name="keep", bufs=1))
+        work = ctx.enter_context(tc.tile_pool(name="work", bufs=2))
+        acts = ctx.enter_context(tc.tile_pool(name="acts", bufs=4))
+        psum = ctx.enter_context(tc.psum_pool(name="psum", bufs=6))
+        psum1 = ctx.enter_context(tc.psum_pool(name="psum1", bufs=1))
+
+        sc = []
+        for m in range(2):
+            plane = keep.tile([P, E, KS, H], U8, name=f"sc{m}", align_bytes=64)
+            sc.append(plane)
+        sc2 = keep.tile([P, E, HS, N], U8, name="sc2", align_bytes=64)
+        for plane in (sc[1], sc2, sc[0]):
+            nc.vector.memset(plane[:].rearrange("p e s i -> p (e s i)").bitcast(I32), 0)
+        xs = []
+        for s in range(KS):
+            plane = keep.tile([P, T], U8, name=f"xs{s}", align_bytes=64)
+            nc.vector.memset(plane[:].bitcast(I32), 0)
+            xs.append(plane)
+
+        win = []
+        for n in range(NB):
+            w = keep.tile([P, T], F32, name=f"win{n}")
+            nc.vector.memset(w[:], 0.0)
+            win.append(w)
+        ident = keep.tile([P, P], F32, name="ident")
+        make_identity(nc, ident[:])
+
+        xf = {}
+
+        def load_x(s, c):
+            a, b = CHUNKS[c]
+            rows = xT[512 * s : 512 * (s + 1), :].rearrange("(p j) t -> p j t", j=4)
+            xf[s, c] = keep.tile([P, 4, b - a], F32, name=f"xf{s}{c}")
+            nc.sync.dma_start(xf[s, c][:], rows[:, :, a:b])
+
+        def load_scales(queue, plane, scales, experts):
+            for q in range(4):
+                queue.dma_start(
+                    plane[32 * q : 32 * q + 4, experts, :, :].rearrange("q e s i -> q (e s) i").bitcast(I32),
+                    scales[experts, :, 4 * q : 4 * q + 4, :].rearrange("e s q i -> q (e s) i").bitcast(I32),
+                )
+
+        wt = {}
+
+        def load_words(e, m, words):
+            wt[e, m] = keep.tile([P, KS, 2 * H], U8, name=f"wt{e}{m}", align_bytes=64)
+            nc.sync.dma_start(wt[e, m][:].bitcast(I32), words[e].rearrange("s p b -> p s b").bitcast(I32))
+
+        load_x(0, 0)
+        load_x(0, 1)
+        offsets = keep.tile([P, SLOTS // 16], U16, name="offsets")
+        nc.sync.dma_start(offsets[:], offs)
+        load_x(1, 0)
+        load_x(1, 1)
+        load_scales(nc.sync, sc[0], w1_scales, slice(0, 2))
+        load_scales(nc.gpsimd, sc[1], w3_scales, slice(0, 2))
+        load_words(0, 0, w1_words)
+        load_words(0, 1, w3_words)
+        load_words(1, 0, w1_words)
+        load_words(1, 1, w3_words)
+        load_scales(nc.sync, sc2, w2_scales, slice(0, 2))
+        wt2 = keep.tile([P, E, HS, 2 * N], U8, name="wt2", align_bytes=64)
+        nc.sync.dma_start(
+            wt2[:].rearrange("p e s b -> p (e s) b").bitcast(I32), w2_words.rearrange("e s p b -> p (e s) b").bitcast(I32)
+        )
+        gates = keep.tile([P, NB, SLOTS], F32, name="gates")
+        nc.sync.dma_start(gates[:], gate.rearrange("(n p) j -> p n j", p=P))
+        resid = keep.tile([P, NB, T], F32, name="resid")
+        nc.sync.dma_start(resid[:], xr.rearrange("(n p) t -> p n t", p=P))
+
+        xq = [keep.tile([P, T], U32, name=f"xq{s}", align_bytes=64) for s in range(KS)]
+        gw, gs = {}, {}
+
+        for e in range(E):
+            for s in range(KS):
+                gw[e, s] = keep.tile([P, C], U32, name=f"gw{e}{s}", align_bytes=64)
+                gs[e, s] = keep.tile([P, C], U8, name=f"gs{e}{s}", align_bytes=64)
+
+        def gather(e, s, a, b):
+            cols = offsets[:, (C * e + a) // 16 : (C * e + b) // 16]
+            nc.vector.tensor_copy(gw[e, s][:, a:b], xq[s][:].indirect(cols))
+            nc.vector.tensor_copy(gs[e, s][:, a:b], xs[s][:].indirect(cols))
+
+        for s in range(KS):
+            xb = keep.tile([P, T, 4], BF16, name=f"xb{s}", align_bytes=64)
+            for a, b, eng in CASTS[s]:
+                c = 0 if b <= CHUNKS[0][1] else 1
+                a0 = CHUNKS[c][0]
+                src = xf[s, c][:, :, a - a0 : b - a0].rearrange("p j t -> p t j")
+                if eng == "v":
+                    nc.vector.tensor_copy(xb[:, a:b, :], src)
+                else:
+                    nc.scalar.copy(xb[:, a:b, :], src)
+            for a, b in QUANTS:
+                nc.vector.quantize_mx(
+                    out=xq[s][:, a:b].bitcast(FP8X4),
+                    scales=xs[s][:, a:b],
+                    in_=xb[:].rearrange("p t j -> p (t j)")[:, 4 * a : 4 * b],
+                )
+            if s == 0:
+                gather(0, 0, 0, C)
+                gather(1, 0, 0, C)
+        gather(0, 1, 0, P)
+        gather(0, 1, P, C)
+        gather(1, 1, 0, C)
+
+        hb = {}
+
+        def layer1(i):
+            e, half = divmod(i, 2)
+            slots = slice(P * half, P * (half + 1))
+            hb[i] = work.tile([P, HS, 512], BF16, name="hb", align_bytes=64)
+            for g in range(HS):
+                banks = []
+                for m in range(2):
+                    acc = psum.tile([P, 512], F32, name="acc")
+                    for s in range(KS):
+                        nc.tensor.matmul_mx(
+                            out=acc[:],
+                            lhsT=gw[e, s][:, slots].bitcast(FP8X4),
+                            lhsT_scale=gs[e, s][:, slots],
+                            rhs=wt[e, m][:, s, 1024 * g : 1024 * (g + 1)].bitcast(FP4X4),
+                            rhs_scale=sc[m][:, e, s, 512 * g : 512 * (g + 1)],
+                            start=(s == 0),
+                            stop=(s == KS - 1),
+                        )
+                    banks.append(acc)
+                order = "p (w u d) -> p u w d"
+                pos = acts.tile([P, 2, P, 2], F32, name="pos")
+                nc.scalar.activation(pos[:], banks[0][:].rearrange(order, u=2, d=2), RELU)
+                nc.vector.tensor_tensor(
+                    hb[i][:, g, :].rearrange("p (u w d) -> p u w d", u=2, d=2),
+                    banks[1][:].rearrange(order, u=2, d=2),
+                    pos[:],
+                    MULT,
+                )
+
+        hq, hs = {}, {}
+
+        def turn(i):
+            words = hb[i][:].rearrange("p g c -> p (g c)").bitcast(F32)
+            turned = psum1.tile([P, HS, 2, P], F32, name="turned")
+            for g in range(HS):
+                for u in range(2):
+                    lo = 256 * g + 128 * u
+                    nc.tensor.transpose(turned[:, g, u, :], words[:, lo : lo + 128], ident[:])
+            ht = work.tile([P, HS * P * 4], BF16, name="ht", align_bytes=64)
+            nc.scalar.copy(
+                ht[:].bitcast(F32).rearrange("p (g r u) -> p g r u", g=HS, u=2),
+                turned[:].rearrange("p g u r -> p g r u"),
+            )
+            hq[i] = work.tile([P, HS * P], U32, name="hq", align_bytes=64)
+            hs[i] = work.tile([P, HS * P], U8, name="hs", align_bytes=64)
+            nc.vector.quantize_mx(out=hq[i][:].bitcast(FP8X4), scales=hs[i][:], in_=ht[:])
+
+        def layer2(i):
+            e = i // 2
+            y = psum1.tile([P, NB, P], F32, name="y")
+            for n in range(NB):
+                for s in range(HS):
+                    nc.tensor.matmul_mx(
+                        out=y[:, n, :],
+                        lhsT=wt2[:, e, s, 2 * P * n : 2 * P * (n + 1)].bitcast(FP4X4),
+                        lhsT_scale=sc2[:, e, s, P * n : P * (n + 1)],
+                        rhs=hq[i][:, P * s : P * (s + 1)].bitcast(FP8X4),
+                        rhs_scale=hs[i][:, P * s : P * (s + 1)],
+                        start=(s == 0),
+                        stop=(s == HS - 1),
+                    )
+            gy = work.tile([P, NB, P], F32, name="gy")
+            nc.vector.tensor_tensor(gy[:], y[:], gates[:, :, P * i : P * (i + 1)], MULT)
+            for n in range(NB):
+                nc.vector.tensor_copy(win[n][:].indirect(offsets[:, 8 * i : 8 * (i + 1)]), gy[:, n, :])
+        def finish(n):
+            total = keep.tile([P, T], F32, name=f"total{n}")
+            engine = nc.gpsimd if n == 0 else nc.vector
+            engine.tensor_tensor(total[:], win[n][:], resid[:, n, :], ADD)
+            nc.sync.dma_start(out[P * n : P * (n + 1), :], total[:])
+
+        layer1(0)
+        layer1(1)
+        turn(0)
+        layer1(2)
+        layer2(0)
+        turn(1)
+        layer1(3)
+        layer2(1)
+        turn(2)
+        layer2(2)
+        turn(3)
+        layer2(3)
+        for n in range(NB):
+            finish(n)

@@ -13,7 +13,6 @@ U16 = mybir.dt.uint16
 U8 = mybir.dt.uint8
 FP8X4 = mybir.dt.float8_e4m3fn_x4
 FP4X4 = mybir.dt.float4_e2m1fn_x4
-COPY = mybir.ActivationFunctionType.Copy
 RELU = mybir.ActivationFunctionType.Relu
 ADD = mybir.AluOpType.add
 MULT = mybir.AluOpType.mult
@@ -24,12 +23,8 @@ KS = K // 512
 HS = H // 512
 NB = N // P
 SLOTS = E * C
-CHUNKS = ((0, 384), (384, 640))
-CASTS = (
-    ((0, 256, "v"), (256, 384, "s"), (384, 512, "v"), (512, 640, "s")),
-    ((0, 256, "s"), (256, 384, "s"), (384, 512, "v"), (512, 640, "s")),
-)
-QUANTS = ((0, 256), (256, 384), (384, 640))
+CHUNKS = (((0, 384), (384, 640)), ((0, 384), (384, 640)))
+BOTH = (0, 1)
 
 
 def tile_moe_res_glu_relu_kernel(
@@ -38,66 +33,60 @@ def tile_moe_res_glu_relu_kernel(
     nc = tc.nc
     with ExitStack() as ctx:
         keep = ctx.enter_context(tc.tile_pool(name="keep", bufs=1))
-        work = ctx.enter_context(tc.tile_pool(name="work", bufs=2))
-        acts = ctx.enter_context(tc.tile_pool(name="acts", bufs=4))
         psum = ctx.enter_context(tc.psum_pool(name="psum", bufs=6))
         psum1 = ctx.enter_context(tc.psum_pool(name="psum1", bufs=1))
 
-        sc = []
-        for m in range(2):
-            plane = keep.tile([P, E, KS, H], U8, name=f"sc{m}", align_bytes=64)
-            sc.append(plane)
-        sc2 = keep.tile([P, E, HS, N], U8, name="sc2", align_bytes=64)
-        for plane in (sc[1], sc2, sc[0]):
-            nc.vector.memset(plane[:].rearrange("p e s i -> p (e s i)").bitcast(I32), 0)
-        xs = []
+        xs, sc = [], []
         for s in range(KS):
             plane = keep.tile([P, T], U8, name=f"xs{s}", align_bytes=64)
             nc.vector.memset(plane[:].bitcast(I32), 0)
             xs.append(plane)
-
+        for m in range(2):
+            plane = keep.tile([P, E, KS, H], U8, name=f"sc{m}", align_bytes=64)
+            nc.vector.memset(plane[:].rearrange("p e s i -> p (e s i)").bitcast(I32), 0)
+            sc.append(plane)
+        sc2 = keep.tile([P, E, HS, N], U8, name="sc2", align_bytes=64)
+        nc.vector.memset(sc2[:].rearrange("p e s i -> p (e s i)").bitcast(I32), 0)
+        ident = keep.tile([P, P], F32, name="ident")
+        make_identity(nc, ident[:])
         win = []
         for n in range(NB):
             w = keep.tile([P, T], F32, name=f"win{n}")
-            nc.vector.memset(w[:], 0.0)
+            nc.gpsimd.memset(w[:], 0.0)
             win.append(w)
-        ident = keep.tile([P, P], F32, name="ident")
-        make_identity(nc, ident[:])
 
-        xf = {}
+        xf, wt = {}, {}
 
         def load_x(s, c):
-            a, b = CHUNKS[c]
+            a, b = CHUNKS[s][c]
             rows = xT[512 * s : 512 * (s + 1), :].rearrange("(p j) t -> p j t", j=4)
             xf[s, c] = keep.tile([P, 4, b - a], F32, name=f"xf{s}{c}")
             nc.sync.dma_start(xf[s, c][:], rows[:, :, a:b])
 
-        def load_scales(queue, plane, scales, experts):
+        def load_scales(plane, scales):
             for q in range(4):
-                queue.dma_start(
-                    plane[32 * q : 32 * q + 4, experts, :, :].rearrange("q e s i -> q (e s) i").bitcast(I32),
-                    scales[experts, :, 4 * q : 4 * q + 4, :].rearrange("e s q i -> q (e s) i").bitcast(I32),
+                nc.sync.dma_start(
+                    plane[32 * q : 32 * q + 4, :, :, :].rearrange("q e s i -> q (e s) i").bitcast(I32),
+                    scales[:, :, 4 * q : 4 * q + 4, :].rearrange("e s q i -> q (e s) i").bitcast(I32),
                 )
-
-        wt = {}
 
         def load_words(e, m, words):
             wt[e, m] = keep.tile([P, KS, 2 * H], U8, name=f"wt{e}{m}", align_bytes=64)
             nc.sync.dma_start(wt[e, m][:].bitcast(I32), words[e].rearrange("s p b -> p s b").bitcast(I32))
 
-        load_x(0, 0)
-        load_x(0, 1)
+        for c in range(len(CHUNKS[0])):
+            load_x(0, c)
         offsets = keep.tile([P, SLOTS // 16], U16, name="offsets")
         nc.sync.dma_start(offsets[:], offs)
-        load_x(1, 0)
-        load_x(1, 1)
-        load_scales(nc.sync, sc[0], w1_scales, slice(0, 2))
-        load_scales(nc.gpsimd, sc[1], w3_scales, slice(0, 2))
+        for c in range(len(CHUNKS[1])):
+            load_x(1, c)
+        load_scales(sc[0], w1_scales)
         load_words(0, 0, w1_words)
         load_words(0, 1, w3_words)
+        load_scales(sc[1], w3_scales)
         load_words(1, 0, w1_words)
         load_words(1, 1, w3_words)
-        load_scales(nc.sync, sc2, w2_scales, slice(0, 2))
+        load_scales(sc2, w2_scales)
         wt2 = keep.tile([P, E, HS, 2 * N], U8, name="wt2", align_bytes=64)
         nc.sync.dma_start(
             wt2[:].rearrange("p e s b -> p (e s) b").bitcast(I32), w2_words.rearrange("e s p b -> p (e s) b").bitcast(I32)
@@ -107,126 +96,204 @@ def tile_moe_res_glu_relu_kernel(
         resid = keep.tile([P, NB, T], F32, name="resid")
         nc.sync.dma_start(resid[:], xr.rearrange("(n p) t -> p n t", p=P))
 
-        xq = [keep.tile([P, T], U32, name=f"xq{s}", align_bytes=64) for s in range(KS)]
-        gw, gs = {}, {}
-
-        for e in range(E):
-            for s in range(KS):
+        xb, xq, gw, gs = [], [], {}, {}
+        for s in range(KS):
+            xb.append(keep.tile([P, T, 4], BF16, name=f"xb{s}", align_bytes=64))
+            xq.append(keep.tile([P, T], U32, name=f"xq{s}", align_bytes=64))
+            for e in range(E):
                 gw[e, s] = keep.tile([P, C], U32, name=f"gw{e}{s}", align_bytes=64)
                 gs[e, s] = keep.tile([P, C], U8, name=f"gs{e}{s}", align_bytes=64)
+
+        def cast(s, a, b, eng):
+            for c, (lo, hi) in enumerate(CHUNKS[s]):
+                if lo <= a and b <= hi:
+                    src = xf[s, c][:, :, a - lo : b - lo].rearrange("p j t -> p t j")
+                    if eng == "V":
+                        nc.vector.tensor_copy(xb[s][:, a:b, :], src)
+                    else:
+                        nc.scalar.copy(xb[s][:, a:b, :], src)
+
+        def quant(s, a, b):
+            nc.vector.quantize_mx(
+                out=xq[s][:, a:b].bitcast(FP8X4),
+                scales=xs[s][:, a:b],
+                in_=xb[s][:].rearrange("p t j -> p (t j)")[:, 4 * a : 4 * b],
+            )
 
         def gather(e, s, a, b):
             cols = offsets[:, (C * e + a) // 16 : (C * e + b) // 16]
             nc.vector.tensor_copy(gw[e, s][:, a:b], xq[s][:].indirect(cols))
             nc.vector.tensor_copy(gs[e, s][:, a:b], xs[s][:].indirect(cols))
 
-        for s in range(KS):
-            xb = keep.tile([P, T, 4], BF16, name=f"xb{s}", align_bytes=64)
-            for a, b, eng in CASTS[s]:
-                c = 0 if b <= CHUNKS[0][1] else 1
-                a0 = CHUNKS[c][0]
-                src = xf[s, c][:, :, a - a0 : b - a0].rearrange("p j t -> p t j")
-                if eng == "v":
-                    nc.vector.tensor_copy(xb[:, a:b, :], src)
-                else:
-                    nc.scalar.copy(xb[:, a:b, :], src)
-            for a, b in QUANTS:
-                nc.vector.quantize_mx(
-                    out=xq[s][:, a:b].bitcast(FP8X4),
-                    scales=xs[s][:, a:b],
-                    in_=xb[:].rearrange("p t j -> p (t j)")[:, 4 * a : 4 * b],
-                )
-            if s == 0:
-                gather(0, 0, 0, C)
-                gather(1, 0, 0, C)
-        gather(0, 1, 0, P)
-        gather(0, 1, P, C)
-        gather(1, 1, 0, C)
+        acc, pos, hb, turned, ht, hq, hs, y, gy = {}, {}, {}, {}, {}, {}, {}, {}, {}
+        for i in range(4):
+            hb[i] = keep.tile([P, HS, 512], BF16, name=f"hb{i}", align_bytes=64)
+            ht[i] = keep.tile([P, HS, P * 4], BF16, name=f"ht{i}", align_bytes=64)
+            hq[i] = keep.tile([P, HS, P], U32, name=f"hq{i}", align_bytes=64)
+            hs[i] = keep.tile([P, HS, P], U8, name=f"hs{i}", align_bytes=64)
+            gy[i] = keep.tile([P, NB, P], F32, name=f"gy{i}")
+            for g in range(HS):
+                pos[i, g] = keep.tile([P, 2, P, 2], F32, name=f"pos{i}{g}")
 
-        hb = {}
-
-        def layer1(i):
+        def mm(m, i, g, passes=BOTH):
             e, half = divmod(i, 2)
             slots = slice(P * half, P * (half + 1))
-            hb[i] = work.tile([P, HS, 512], BF16, name="hb", align_bytes=64)
-            for g in range(HS):
-                banks = []
-                for m in range(2):
-                    acc = psum.tile([P, 512], F32, name="acc")
-                    for s in range(KS):
-                        nc.tensor.matmul_mx(
-                            out=acc[:],
-                            lhsT=gw[e, s][:, slots].bitcast(FP8X4),
-                            lhsT_scale=gs[e, s][:, slots],
-                            rhs=wt[e, m][:, s, 1024 * g : 1024 * (g + 1)].bitcast(FP4X4),
-                            rhs_scale=sc[m][:, e, s, 512 * g : 512 * (g + 1)],
-                            start=(s == 0),
-                            stop=(s == KS - 1),
-                        )
-                    banks.append(acc)
-                order = "p (w u d) -> p u w d"
-                pos = acts.tile([P, 2, P, 2], F32, name="pos")
-                nc.scalar.activation(pos[:], banks[0][:].rearrange(order, u=2, d=2), RELU)
-                nc.vector.tensor_tensor(
-                    hb[i][:, g, :].rearrange("p (u w d) -> p u w d", u=2, d=2),
-                    banks[1][:].rearrange(order, u=2, d=2),
-                    pos[:],
-                    MULT,
+            if 0 in passes:
+                acc[m, i, g] = psum.tile([P, 512], F32, name="acc")
+            for s in passes:
+                nc.tensor.matmul_mx(
+                    out=acc[m, i, g][:],
+                    lhsT=gw[e, s][:, slots].bitcast(FP8X4),
+                    lhsT_scale=gs[e, s][:, slots],
+                    rhs=wt[e, m][:, s, 1024 * g : 1024 * (g + 1)].bitcast(FP4X4),
+                    rhs_scale=sc[m][:, e, s, 512 * g : 512 * (g + 1)],
+                    start=(s == 0),
+                    stop=(s == KS - 1),
                 )
 
-        hq, hs = {}, {}
+        def relu(i, g):
+            nc.scalar.activation(pos[i, g][:], acc[0, i, g][:].rearrange("p (w u d) -> p u w d", u=2, d=2), RELU)
 
-        def turn(i):
-            words = hb[i][:].rearrange("p g c -> p (g c)").bitcast(F32)
-            turned = psum1.tile([P, HS, 2, P], F32, name="turned")
-            for g in range(HS):
-                for u in range(2):
-                    lo = 256 * g + 128 * u
-                    nc.tensor.transpose(turned[:, g, u, :], words[:, lo : lo + 128], ident[:])
-            ht = work.tile([P, HS * P * 4], BF16, name="ht", align_bytes=64)
-            nc.scalar.copy(
-                ht[:].bitcast(F32).rearrange("p (g r u) -> p g r u", g=HS, u=2),
-                turned[:].rearrange("p g u r -> p g r u"),
+        def prod(i, g, halves=BOTH):
+            us = slice(halves[0], halves[-1] + 1)
+            nc.vector.tensor_tensor(
+                hb[i][:, g, :].rearrange("p (u w d) -> p u w d", u=2, d=2)[:, us],
+                acc[1, i, g][:].rearrange("p (w u d) -> p u w d", u=2, d=2)[:, us],
+                pos[i, g][:, us],
+                MULT,
             )
-            hq[i] = work.tile([P, HS * P], U32, name="hq", align_bytes=64)
-            hs[i] = work.tile([P, HS * P], U8, name="hs", align_bytes=64)
-            nc.vector.quantize_mx(out=hq[i][:].bitcast(FP8X4), scales=hs[i][:], in_=ht[:])
+
+        def turn(i, gs_=BOTH):
+            if gs_ == (1,):
+                bank = psum.tile([P, 2, P], F32, name="acc")
+            else:
+                bank = psum1.tile([P, HS, 2, P], F32, name="turned")
+            for k, g in enumerate(gs_):
+                words = hb[i][:, g, :].bitcast(F32)
+                for u in range(2):
+                    dst = bank[:, u, :] if gs_ == (1,) else bank[:, k, u, :]
+                    nc.tensor.transpose(dst, words[:, P * u : P * (u + 1)], ident[:])
+            src = bank[:].rearrange("p u r -> p r u") if gs_ == (1,) else bank[:, : len(gs_)].rearrange("p g u r -> p g r u")
+            lo = gs_[0]
+            dst = ht[i][:, lo : lo + len(gs_), :].rearrange("p g c -> p (g c)").bitcast(F32)
+            if gs_ == (1,):
+                dst = dst.rearrange("p (r u) -> p r u", u=2)
+            else:
+                dst = dst.rearrange("p (g r u) -> p g r u", g=len(gs_), u=2)
+            nc.scalar.copy(dst, src)
+
+        def quant_h(i, gs_=BOTH):
+            g = slice(gs_[0], gs_[-1] + 1)
+            nc.vector.quantize_mx(
+                out=hq[i][:, g, :].rearrange("p g r -> p (g r)").bitcast(FP8X4),
+                scales=hs[i][:, g, :].rearrange("p g r -> p (g r)"),
+                in_=ht[i][:, g, :].rearrange("p g c -> p (g c)"),
+            )
+
+        def second(i, n, s, dst):
+            e = i // 2
+            nc.tensor.matmul_mx(
+                out=dst,
+                lhsT=wt2[:, e, s, 2 * P * n : 2 * P * (n + 1)].bitcast(FP4X4),
+                lhsT_scale=sc2[:, e, s, P * n : P * (n + 1)],
+                rhs=hq[i][:, s, :].bitcast(FP8X4),
+                rhs_scale=hs[i][:, s, :],
+                start=(s == 0),
+                stop=(s == HS - 1),
+            )
 
         def layer2(i):
-            e = i // 2
-            y = psum1.tile([P, NB, P], F32, name="y")
+            y[i] = psum1.tile([P, NB, P], F32, name="y")
             for n in range(NB):
                 for s in range(HS):
-                    nc.tensor.matmul_mx(
-                        out=y[:, n, :],
-                        lhsT=wt2[:, e, s, 2 * P * n : 2 * P * (n + 1)].bitcast(FP4X4),
-                        lhsT_scale=sc2[:, e, s, P * n : P * (n + 1)],
-                        rhs=hq[i][:, P * s : P * (s + 1)].bitcast(FP8X4),
-                        rhs_scale=hs[i][:, P * s : P * (s + 1)],
-                        start=(s == 0),
-                        stop=(s == HS - 1),
-                    )
-            gy = work.tile([P, NB, P], F32, name="gy")
-            nc.vector.tensor_tensor(gy[:], y[:], gates[:, :, P * i : P * (i + 1)], MULT)
-            for n in range(NB):
-                nc.vector.tensor_copy(win[n][:].indirect(offsets[:, 8 * i : 8 * (i + 1)]), gy[:, n, :])
-        def finish(n):
-            total = keep.tile([P, T], F32, name=f"total{n}")
-            engine = nc.gpsimd if n == 0 else nc.vector
-            engine.tensor_tensor(total[:], win[n][:], resid[:, n, :], ADD)
-            nc.sync.dma_start(out[P * n : P * (n + 1), :], total[:])
+                    second(i, n, s, y[i][:, n, :])
+            nc.scalar.copy(gy[i][:], y[i][:])
 
-        layer1(0)
-        layer1(1)
+        def scatter(i, n):
+            window = win[n][:].indirect(offsets[:, 8 * i : 8 * (i + 1)])
+            nc.vector.tensor_tensor(window, gy[i][:, n, :], gates[:, n, P * i : P * (i + 1)], MULT)
+
+        def last(i):
+            banks = [psum1.tile([P, P], F32, name="y"), psum.tile([P, P], F32, name="acc")]
+            for s in range(HS):
+                for n in range(NB):
+                    second(i, n, s, banks[n][:])
+            for n in range(NB):
+                if n == 1:
+                    scatter(2, 1)
+                nc.vector.tensor_tensor(gy[i][:, n, :], banks[n][:], gates[:, n, P * i : P * (i + 1)], MULT)
+                nc.vector.tensor_copy(win[n][:].indirect(offsets[:, 8 * i : 8 * (i + 1)]), gy[i][:, n, :])
+                total = keep.tile([P, T], F32, name=f"total{n}")
+                engine = nc.gpsimd if n == 0 else nc.vector
+                engine.tensor_tensor(total[:], win[n][:], resid[:, n, :], ADD)
+                nc.sync.dma_start(out[P * n : P * (n + 1), :], total[:])
+
+        cast(0, 0, 128, "S")
+        cast(0, 128, 256, "V")
+        cast(0, 256, 384, "V")
+        quant(0, 0, 256)
+        quant(0, 256, 384)
+        cast(0, 384, 512, "S")
+        cast(0, 512, 640, "V")
+        quant(0, 384, 640)
+        gather(0, 0, 0, C)
+        cast(1, 0, 256, "S")
+        cast(1, 256, 384, "V")
+        quant(1, 256, 384)
+        quant(1, 0, 256)
+        cast(1, 384, 512, "V")
+        cast(1, 512, 640, "S")
+        quant(1, 384, 640)
+        gather(0, 1, 0, P)
+        first = ((0, 0, 0), (0, 0, 1), (0, 1, 0), (0, 1, 1), (1, 0, 0), (1, 0, 1))
+        for s in range(KS):
+            if s == 1:
+                gather(0, 1, P, C)
+            for m, i, g in first:
+                mm(m, i, g, (s,))
+                if m == 0 and s == 1:
+                    relu(i, g)
+        gather(1, 0, 0, C)
+        gather(1, 1, 0, C)
+        prod(0, 0)
+        mm(1, 1, 0)
+        prod(0, 1)
+        mm(1, 1, 1)
         turn(0)
-        layer1(2)
-        layer2(0)
+        prod(1, 0)
+        mm(0, 2, 0)
+        mm(0, 2, 1)
+        relu(2, 0)
+        relu(2, 1)
+        prod(1, 1)
+        quant_h(0)
         turn(1)
-        layer1(3)
+        mm(1, 2, 0)
+        prod(2, 0)
+        mm(1, 2, 1)
+        layer2(0)
+        quant_h(1)
+        prod(2, 1)
+        mm(0, 3, 0)
+        mm(0, 3, 1)
+        relu(3, 0)
+        relu(3, 1)
+        scatter(0, 0)
         layer2(1)
+        mm(1, 3, 0)
+        prod(3, 0)
         turn(2)
+        scatter(0, 1)
+        mm(1, 3, 1)
+        prod(3, 1, (0,))
+        prod(3, 1, (1,))
+        quant_h(2)
+        turn(3, (0,))
+        quant_h(3, (0,))
+        scatter(1, 0)
         layer2(2)
-        turn(3)
-        layer2(3)
-        for n in range(NB):
-            finish(n)
+        turn(3, (1,))
+        quant_h(3, (1,))
+        scatter(1, 1)
+        scatter(2, 0)
+        last(3)

@@ -207,11 +207,11 @@ def tile_moe_res_glu_relu_kernel(
             for n in range(NB):
                 for s in range(HS):
                     second(i, n, s, y[i][:, n, :])
-            nc.scalar.copy(gy[i][:], y[i][:])
+            nc.vector.tensor_tensor(gy[i][:], y[i][:], gates[:, :, P * i : P * (i + 1)], MULT)
 
         def scatter(i, n):
             window = win[n][:].indirect(offsets[:, 8 * i : 8 * (i + 1)])
-            nc.vector.tensor_tensor(window, gy[i][:, n, :], gates[:, n, P * i : P * (i + 1)], MULT)
+            nc.vector.tensor_copy(window, gy[i][:, n, :])
 
         def last(i):
             banks = [psum1.tile([P, P], F32, name="y"), psum.tile([P, P], F32, name="acc")]

@@ -23,7 +23,7 @@ KS = K // 512
 HS = H // 512
 NB = N // P
 SLOTS = E * C
-CHUNKS = (((0, 384), (384, 640)), ((0, 384), (384, 640)))
+CHUNKS = (((0, 640),), ((0, 640),))
 BOTH = (0, 1)
 
 
@@ -41,10 +41,11 @@ def tile_moe_res_glu_relu_kernel(
             plane = keep.tile([P, T], U8, name=f"xs{s}", align_bytes=64)
             nc.vector.memset(plane[:].bitcast(I32), 0)
             xs.append(plane)
-        for m in range(2):
-            plane = keep.tile([P, E, KS, H], U8, name=f"sc{m}", align_bytes=64)
-            nc.vector.memset(plane[:].rearrange("p e s i -> p (e s i)").bitcast(I32), 0)
-            sc.append(plane)
+        for e in range(E):
+            for m in range(2):
+                plane = keep.tile([P, KS, H], U8, name=f"sc{e}{m}", align_bytes=64)
+                nc.vector.memset(plane[:].rearrange("p s i -> p (s i)").bitcast(I32), 0)
+                sc.append(plane)
         sc2 = keep.tile([P, E, HS, N], U8, name="sc2", align_bytes=64)
         nc.vector.memset(sc2[:].rearrange("p e s i -> p (e s i)").bitcast(I32), 0)
         ident = keep.tile([P, P], F32, name="ident")
@@ -63,11 +64,11 @@ def tile_moe_res_glu_relu_kernel(
             xf[s, c] = keep.tile([P, 4, b - a], F32, name=f"xf{s}{c}")
             nc.sync.dma_start(xf[s, c][:], rows[:, :, a:b])
 
-        def load_scales(plane, scales):
+        def load_scales(e, m, scales):
             for q in range(4):
                 nc.sync.dma_start(
-                    plane[32 * q : 32 * q + 4, :, :, :].rearrange("q e s i -> q (e s) i").bitcast(I32),
-                    scales[:, :, 4 * q : 4 * q + 4, :].rearrange("e s q i -> q (e s) i").bitcast(I32),
+                    sc[2 * e + m][32 * q : 32 * q + 4, :, :].bitcast(I32),
+                    scales[e, :, 4 * q : 4 * q + 4, :].rearrange("s q i -> q s i").bitcast(I32),
                 )
 
         def load_words(e, m, words):
@@ -80,17 +81,23 @@ def tile_moe_res_glu_relu_kernel(
         nc.sync.dma_start(offsets[:], offs)
         for c in range(len(CHUNKS[1])):
             load_x(1, c)
-        load_scales(sc[0], w1_scales)
+        load_scales(0, 0, w1_scales)
         load_words(0, 0, w1_words)
         load_words(0, 1, w3_words)
-        load_scales(sc[1], w3_scales)
+        load_scales(0, 1, w3_scales)
         load_words(1, 0, w1_words)
         load_words(1, 1, w3_words)
-        load_scales(sc2, w2_scales)
+        load_scales(1, 0, w1_scales)
         wt2 = keep.tile([P, E, HS, 2 * N], U8, name="wt2", align_bytes=64)
         nc.sync.dma_start(
             wt2[:].rearrange("p e s b -> p (e s) b").bitcast(I32), w2_words.rearrange("e s p b -> p (e s) b").bitcast(I32)
         )
+        load_scales(1, 1, w3_scales)
+        for q in range(4):
+            nc.sync.dma_start(
+                sc2[32 * q : 32 * q + 4, :, :, :].rearrange("q e s i -> q (e s) i").bitcast(I32),
+                w2_scales[:, :, 4 * q : 4 * q + 4, :].rearrange("e s q i -> q (e s) i").bitcast(I32),
+            )
         gates = keep.tile([P, NB, SLOTS], F32, name="gates")
         nc.sync.dma_start(gates[:], gate.rearrange("(n p) j -> p n j", p=P))
         resid = keep.tile([P, NB, T], F32, name="resid")
@@ -146,7 +153,7 @@ def tile_moe_res_glu_relu_kernel(
                     lhsT=gw[e, s][:, slots].bitcast(FP8X4),
                     lhsT_scale=gs[e, s][:, slots],
                     rhs=wt[e, m][:, s, 1024 * g : 1024 * (g + 1)].bitcast(FP4X4),
-                    rhs_scale=sc[m][:, e, s, 512 * g : 512 * (g + 1)],
+                    rhs_scale=sc[2 * e + m][:, s, 512 * g : 512 * (g + 1)],
                     start=(s == 0),
                     stop=(s == KS - 1),
                 )
@@ -207,26 +214,17 @@ def tile_moe_res_glu_relu_kernel(
             for n in range(NB):
                 for s in range(HS):
                     second(i, n, s, y[i][:, n, :])
-            nc.vector.tensor_tensor(gy[i][:], y[i][:], gates[:, :, P * i : P * (i + 1)], MULT)
+            nc.scalar.copy(gy[i][:], y[i][:])
 
         def scatter(i, n):
             window = win[n][:].indirect(offsets[:, 8 * i : 8 * (i + 1)])
-            nc.vector.tensor_copy(window, gy[i][:, n, :])
+            nc.vector.tensor_tensor(window, gy[i][:, n, :], gates[:, n, P * i : P * (i + 1)], MULT)
 
-        def last(i):
-            banks = [psum1.tile([P, P], F32, name="y"), psum.tile([P, P], F32, name="acc")]
-            for s in range(HS):
-                for n in range(NB):
-                    second(i, n, s, banks[n][:])
-            for n in range(NB):
-                if n == 1:
-                    scatter(2, 1)
-                nc.vector.tensor_tensor(gy[i][:, n, :], banks[n][:], gates[:, n, P * i : P * (i + 1)], MULT)
-                nc.vector.tensor_copy(win[n][:].indirect(offsets[:, 8 * i : 8 * (i + 1)]), gy[i][:, n, :])
-                total = keep.tile([P, T], F32, name=f"total{n}")
-                engine = nc.gpsimd if n == 0 else nc.vector
-                engine.tensor_tensor(total[:], win[n][:], resid[:, n, :], ADD)
-                nc.sync.dma_start(out[P * n : P * (n + 1), :], total[:])
+        total = [keep.tile([P, T], F32, name=f"total{n}") for n in range(NB)]
+
+        def finish(n, a, b):
+            nc.vector.tensor_tensor(total[n][:, a:b], win[n][:, a:b], resid[:, n, a:b], ADD)
+            nc.sync.dma_start(out[P * n : P * (n + 1), a:b], total[n][:, a:b])
 
         cast(0, 0, 128, "S")
         cast(0, 128, 256, "V")
@@ -244,11 +242,9 @@ def tile_moe_res_glu_relu_kernel(
         cast(1, 384, 512, "V")
         cast(1, 512, 640, "S")
         quant(1, 384, 640)
-        gather(0, 1, 0, P)
+        gather(0, 1, 0, C)
         first = ((0, 0, 0), (0, 0, 1), (0, 1, 0), (0, 1, 1), (1, 0, 0), (1, 0, 1))
         for s in range(KS):
-            if s == 1:
-                gather(0, 1, P, C)
             for m, i, g in first:
                 mm(m, i, g, (s,))
                 if m == 0 and s == 1:
@@ -285,15 +281,18 @@ def tile_moe_res_glu_relu_kernel(
         turn(2)
         scatter(0, 1)
         mm(1, 3, 1)
-        prod(3, 1, (0,))
-        prod(3, 1, (1,))
+        prod(3, 1)
         quant_h(2)
-        turn(3, (0,))
-        quant_h(3, (0,))
+        turn(3)
         scatter(1, 0)
         layer2(2)
-        turn(3, (1,))
-        quant_h(3, (1,))
         scatter(1, 1)
+        quant_h(3)
         scatter(2, 0)
-        last(3)
+        layer2(3)
+        scatter(3, 0)
+        finish(0, 0, T)
+        scatter(2, 1)
+        scatter(3, 1)
+        finish(1, 0, T // 2)
+        finish(1, T // 2, T)

@@ -41,11 +41,10 @@ def tile_moe_res_glu_relu_kernel(
             plane = keep.tile([P, T], U8, name=f"xs{s}", align_bytes=64)
             nc.vector.memset(plane[:].bitcast(I32), 0)
             xs.append(plane)
-        for e in range(E):
-            for m in range(2):
-                plane = keep.tile([P, KS, H], U8, name=f"sc{e}{m}", align_bytes=64)
-                nc.vector.memset(plane[:].rearrange("p s i -> p (s i)").bitcast(I32), 0)
-                sc.append(plane)
+        for m in range(2):
+            plane = keep.tile([P, E, KS, H], U8, name=f"sc{m}", align_bytes=64)
+            nc.vector.memset(plane[:].rearrange("p e s i -> p (e s i)").bitcast(I32), 0)
+            sc.append(plane)
         sc2 = keep.tile([P, E, HS, N], U8, name="sc2", align_bytes=64)
         nc.vector.memset(sc2[:].rearrange("p e s i -> p (e s i)").bitcast(I32), 0)
         ident = keep.tile([P, P], F32, name="ident")
@@ -64,11 +63,11 @@ def tile_moe_res_glu_relu_kernel(
             xf[s, c] = keep.tile([P, 4, b - a], F32, name=f"xf{s}{c}")
             nc.sync.dma_start(xf[s, c][:], rows[:, :, a:b])
 
-        def load_scales(e, m, scales):
+        def load_scales(plane, scales):
             for q in range(4):
                 nc.sync.dma_start(
-                    sc[2 * e + m][32 * q : 32 * q + 4, :, :].bitcast(I32),
-                    scales[e, :, 4 * q : 4 * q + 4, :].rearrange("s q i -> q s i").bitcast(I32),
+                    plane[32 * q : 32 * q + 4, :, :, :].rearrange("q e s i -> q (e s) i").bitcast(I32),
+                    scales[:, :, 4 * q : 4 * q + 4, :].rearrange("e s q i -> q (e s) i").bitcast(I32),
                 )
 
         def load_words(e, m, words):
@@ -81,23 +80,17 @@ def tile_moe_res_glu_relu_kernel(
         nc.sync.dma_start(offsets[:], offs)
         for c in range(len(CHUNKS[1])):
             load_x(1, c)
-        load_scales(0, 0, w1_scales)
+        load_scales(sc[0], w1_scales)
         load_words(0, 0, w1_words)
         load_words(0, 1, w3_words)
-        load_scales(0, 1, w3_scales)
+        load_scales(sc[1], w3_scales)
         load_words(1, 0, w1_words)
         load_words(1, 1, w3_words)
-        load_scales(1, 0, w1_scales)
+        load_scales(sc2, w2_scales)
         wt2 = keep.tile([P, E, HS, 2 * N], U8, name="wt2", align_bytes=64)
         nc.sync.dma_start(
             wt2[:].rearrange("p e s b -> p (e s) b").bitcast(I32), w2_words.rearrange("e s p b -> p (e s) b").bitcast(I32)
         )
-        load_scales(1, 1, w3_scales)
-        for q in range(4):
-            nc.sync.dma_start(
-                sc2[32 * q : 32 * q + 4, :, :, :].rearrange("q e s i -> q (e s) i").bitcast(I32),
-                w2_scales[:, :, 4 * q : 4 * q + 4, :].rearrange("e s q i -> q (e s) i").bitcast(I32),
-            )
         gates = keep.tile([P, NB, SLOTS], F32, name="gates")
         nc.sync.dma_start(gates[:], gate.rearrange("(n p) j -> p n j", p=P))
         resid = keep.tile([P, NB, T], F32, name="resid")
@@ -153,7 +146,7 @@ def tile_moe_res_glu_relu_kernel(
                     lhsT=gw[e, s][:, slots].bitcast(FP8X4),
                     lhsT_scale=gs[e, s][:, slots],
                     rhs=wt[e, m][:, s, 1024 * g : 1024 * (g + 1)].bitcast(FP4X4),
-                    rhs_scale=sc[2 * e + m][:, s, 512 * g : 512 * (g + 1)],
+                    rhs_scale=sc[m][:, e, s, 512 * g : 512 * (g + 1)],
                     start=(s == 0),
                     stop=(s == KS - 1),
                 )
@@ -227,20 +220,19 @@ def tile_moe_res_glu_relu_kernel(
             nc.sync.dma_start(out[P * n : P * (n + 1), a:b], total[n][:, a:b])
 
         cast(0, 0, 128, "S")
-        cast(0, 128, 256, "V")
-        cast(0, 256, 384, "V")
-        quant(0, 0, 256)
-        quant(0, 256, 384)
+        cast(0, 128, 384, "V")
         cast(0, 384, 512, "S")
         cast(0, 512, 640, "V")
+        quant(0, 0, 256)
+        quant(0, 256, 384)
         quant(0, 384, 640)
         gather(0, 0, 0, C)
-        cast(1, 0, 256, "S")
-        cast(1, 256, 384, "V")
-        quant(1, 256, 384)
+        cast(1, 0, 128, "S")
+        cast(1, 128, 384, "V")
+        cast(1, 384, 512, "S")
+        cast(1, 512, 640, "V")
         quant(1, 0, 256)
-        cast(1, 384, 512, "V")
-        cast(1, 512, 640, "S")
+        quant(1, 256, 384)
         quant(1, 384, 640)
         gather(0, 1, 0, C)
         first = ((0, 0, 0), (0, 0, 1), (0, 1, 0), (0, 1, 1), (1, 0, 0), (1, 0, 1))

from contextlib import ExitStack

import concourse.mybir as mybir
from concourse.masks import make_identity

FLOPS = 2 * 512 * (1024 * 1024 * 2 + 1024 * 256)

F32 = mybir.dt.float32
BF16 = mybir.dt.bfloat16
U32 = mybir.dt.uint32
I32 = mybir.dt.int32
U16 = mybir.dt.uint16
U8 = mybir.dt.uint8
FP8X4 = mybir.dt.float8_e4m3fn_x4
FP4X4 = mybir.dt.float4_e2m1fn_x4
RELU = mybir.ActivationFunctionType.Relu
ADD = mybir.AluOpType.add
MULT = mybir.AluOpType.mult

P = 128
K, T, E, C, H, N = 1024, 640, 2, 256, 1024, 256
KS = K // 512
HS = H // 512
NB = N // P
SLOTS = E * C
CHUNKS = (((0, 640),), ((0, 640),))
BOTH = (0, 1)


def tile_moe_res_glu_relu_kernel(
    tc, xT, xr, w1_words, w1_scales, w3_words, w3_scales, w2_words, w2_scales, gate, offs, out
):
    nc = tc.nc
    with ExitStack() as ctx:
        keep = ctx.enter_context(tc.tile_pool(name="keep", bufs=1))
        psum = ctx.enter_context(tc.psum_pool(name="psum", bufs=6))
        psum1 = ctx.enter_context(tc.psum_pool(name="psum1", bufs=1))

        xs, sc = [], []
        for s in range(KS):
            plane = keep.tile([P, T], U8, name=f"xs{s}", align_bytes=64)
            nc.vector.memset(plane[:].bitcast(I32), 0)
            xs.append(plane)
        for m in range(2):
            plane = keep.tile([P, E, KS, H], U8, name=f"sc{m}", align_bytes=64)
            nc.vector.memset(plane[:].rearrange("p e s i -> p (e s i)").bitcast(I32), 0)
            sc.append(plane)
        sc2 = keep.tile([P, E, HS, N], U8, name="sc2", align_bytes=64)
        nc.vector.memset(sc2[:].rearrange("p e s i -> p (e s i)").bitcast(I32), 0)
        ident = keep.tile([P, P], F32, name="ident")
        make_identity(nc, ident[:])
        win = []
        for n in range(NB):
            w = keep.tile([P, T], F32, name=f"win{n}")
            nc.gpsimd.memset(w[:], 0.0)
            win.append(w)

        xf, wt = {}, {}

        def load_x(s, c):
            a, b = CHUNKS[s][c]
            rows = xT[512 * s : 512 * (s + 1), :].rearrange("(p j) t -> p j t", j=4)
            xf[s, c] = keep.tile([P, 4, b - a], F32, name=f"xf{s}{c}")
            nc.sync.dma_start(xf[s, c][:], rows[:, :, a:b])

        def load_scales(plane, scales):
            for q in range(4):
                nc.sync.dma_start(
                    plane[32 * q : 32 * q + 4, :, :, :].rearrange("q e s i -> q (e s) i").bitcast(I32),
                    scales[:, :, 4 * q : 4 * q + 4, :].rearrange("e s q i -> q (e s) i").bitcast(I32),
                )

        def load_words(e, m, words):
            wt[e, m] = keep.tile([P, KS, 2 * H], U8, name=f"wt{e}{m}", align_bytes=64)
            nc.sync.dma_start(wt[e, m][:].bitcast(I32), words[e].rearrange("s p b -> p s b").bitcast(I32))

        for c in range(len(CHUNKS[0])):
            load_x(0, c)
        offsets = keep.tile([P, SLOTS // 16], U16, name="offsets")
        nc.sync.dma_start(offsets[:], offs)
        for c in range(len(CHUNKS[1])):
            load_x(1, c)
        load_scales(sc[0], w1_scales)
        load_words(0, 0, w1_words)
        load_words(0, 1, w3_words)
        load_scales(sc[1], w3_scales)
        load_words(1, 0, w1_words)
        load_words(1, 1, w3_words)
        load_scales(sc2, w2_scales)
        wt2 = keep.tile([P, E, HS, 2 * N], U8, name="wt2", align_bytes=64)
        nc.sync.dma_start(
            wt2[:].rearrange("p e s b -> p (e s) b").bitcast(I32), w2_words.rearrange("e s p b -> p (e s) b").bitcast(I32)
        )
        gates = keep.tile([P, NB, SLOTS], F32, name="gates")
        nc.sync.dma_start(gates[:], gate.rearrange("(n p) j -> p n j", p=P))
        resid = keep.tile([P, NB, T], F32, name="resid")
        nc.sync.dma_start(resid[:], xr.rearrange("(n p) t -> p n t", p=P))

        xb, xq, gw, gs = [], [], {}, {}
        for s in range(KS):
            xb.append(keep.tile([P, T, 4], BF16, name=f"xb{s}", align_bytes=64))
            xq.append(keep.tile([P, T], U32, name=f"xq{s}", align_bytes=64))
            for e in range(E):
                gw[e, s] = keep.tile([P, C], U32, name=f"gw{e}{s}", align_bytes=64)
                gs[e, s] = keep.tile([P, C], U8, name=f"gs{e}{s}", align_bytes=64)

        def cast(s, a, b, eng):
            for c, (lo, hi) in enumerate(CHUNKS[s]):
                if lo <= a and b <= hi:
                    src = xf[s, c][:, :, a - lo : b - lo].rearrange("p j t -> p t j")
                    if eng == "V":
                        nc.vector.tensor_copy(xb[s][:, a:b, :], src)
                    else:
                        nc.scalar.copy(xb[s][:, a:b, :], src)

        def quant(s, a, b):
            nc.vector.quantize_mx(
                out=xq[s][:, a:b].bitcast(FP8X4),
                scales=xs[s][:, a:b],
                in_=xb[s][:].rearrange("p t j -> p (t j)")[:, 4 * a : 4 * b],
            )

        def gather(e, s, a, b):
            cols = offsets[:, (C * e + a) // 16 : (C * e + b) // 16]
            nc.vector.tensor_copy(gw[e, s][:, a:b], xq[s][:].indirect(cols))
            nc.vector.tensor_copy(gs[e, s][:, a:b], xs[s][:].indirect(cols))

        acc, pos, hb, turned, ht, hq, hs, y, gy = {}, {}, {}, {}, {}, {}, {}, {}, {}
        for i in range(4):
            hb[i] = keep.tile([P, HS, 512], BF16, name=f"hb{i}", align_bytes=64)
            ht[i] = keep.tile([P, HS, P * 4], BF16, name=f"ht{i}", align_bytes=64)
            hq[i] = keep.tile([P, HS, P], U32, name=f"hq{i}", align_bytes=64)
            hs[i] = keep.tile([P, HS, P], U8, name=f"hs{i}", align_bytes=64)
            gy[i] = keep.tile([P, NB, P], F32, name=f"gy{i}")
            for g in range(HS):
                pos[i, g] = keep.tile([P, 2, P, 2], F32, name=f"pos{i}{g}")

        def mm(m, i, g, passes=BOTH):
            e, half = divmod(i, 2)
            slots = slice(P * half, P * (half + 1))
            if 0 in passes:
                acc[m, i, g] = psum.tile([P, 512], F32, name="acc")
            for s in passes:
                nc.tensor.matmul_mx(
                    out=acc[m, i, g][:],
                    lhsT=gw[e, s][:, slots].bitcast(FP8X4),
                    lhsT_scale=gs[e, s][:, slots],
                    rhs=wt[e, m][:, s, 1024 * g : 1024 * (g + 1)].bitcast(FP4X4),
                    rhs_scale=sc[m][:, e, s, 512 * g : 512 * (g + 1)],
                    start=(s == 0),
                    stop=(s == KS - 1),
                )

        def relu(i, g):
            nc.scalar.activation(pos[i, g][:], acc[0, i, g][:].rearrange("p (w u d) -> p u w d", u=2, d=2), RELU)

        def prod(i, g, halves=BOTH):
            us = slice(halves[0], halves[-1] + 1)
            nc.vector.tensor_tensor(
                hb[i][:, g, :].rearrange("p (u w d) -> p u w d", u=2, d=2)[:, us],
                acc[1, i, g][:].rearrange("p (w u d) -> p u w d", u=2, d=2)[:, us],
                pos[i, g][:, us],
                MULT,
            )

        def turn(i, gs_=BOTH):
            if gs_ == (1,):
                bank = psum.tile([P, 2, P], F32, name="acc")
            else:
                bank = psum1.tile([P, HS, 2, P], F32, name="turned")
            for k, g in enumerate(gs_):
                words = hb[i][:, g, :].bitcast(F32)
                for u in range(2):
                    dst = bank[:, u, :] if gs_ == (1,) else bank[:, k, u, :]
                    nc.tensor.transpose(dst, words[:, P * u : P * (u + 1)], ident[:])
            src = bank[:].rearrange("p u r -> p r u") if gs_ == (1,) else bank[:, : len(gs_)].rearrange("p g u r -> p g r u")
            lo = gs_[0]
            dst = ht[i][:, lo : lo + len(gs_), :].rearrange("p g c -> p (g c)").bitcast(F32)
            if gs_ == (1,):
                dst = dst.rearrange("p (r u) -> p r u", u=2)
            else:
                dst = dst.rearrange("p (g r u) -> p g r u", g=len(gs_), u=2)
            nc.scalar.copy(dst, src)

        def quant_h(i, gs_=BOTH):
            g = slice(gs_[0], gs_[-1] + 1)
            nc.vector.quantize_mx(
                out=hq[i][:, g, :].rearrange("p g r -> p (g r)").bitcast(FP8X4),
                scales=hs[i][:, g, :].rearrange("p g r -> p (g r)"),
                in_=ht[i][:, g, :].rearrange("p g c -> p (g c)"),
            )

        def second(i, n, s, dst):
            e = i // 2
            nc.tensor.matmul_mx(
                out=dst,
                lhsT=wt2[:, e, s, 2 * P * n : 2 * P * (n + 1)].bitcast(FP4X4),
                lhsT_scale=sc2[:, e, s, P * n : P * (n + 1)],
                rhs=hq[i][:, s, :].bitcast(FP8X4),
                rhs_scale=hs[i][:, s, :],
                start=(s == 0),
                stop=(s == HS - 1),
            )

        def layer2(i):
            y[i] = psum1.tile([P, NB, P], F32, name="y")
            for n in range(NB):
                for s in range(HS):
                    second(i, n, s, y[i][:, n, :])
            nc.scalar.copy(gy[i][:], y[i][:])

        def scatter(i, n):
            window = win[n][:].indirect(offsets[:, 8 * i : 8 * (i + 1)])
            nc.vector.tensor_tensor(window, gy[i][:, n, :], gates[:, n, P * i : P * (i + 1)], MULT)

        total = [keep.tile([P, T], F32, name=f"total{n}") for n in range(NB)]

        def finish(n, a, b):
            nc.vector.tensor_tensor(total[n][:, a:b], win[n][:, a:b], resid[:, n, a:b], ADD)
            nc.sync.dma_start(out[P * n : P * (n + 1), a:b], total[n][:, a:b])

        cast(0, 0, 128, "S")
        cast(0, 128, 384, "V")
        cast(0, 384, 512, "S")
        cast(0, 512, 640, "V")
        quant(0, 0, 256)
        quant(0, 256, 384)
        quant(0, 384, 640)
        gather(0, 0, 0, C)
        cast(1, 0, 128, "S")
        cast(1, 128, 384, "V")
        cast(1, 384, 512, "S")
        cast(1, 512, 640, "V")
        quant(1, 0, 256)
        quant(1, 256, 384)
        quant(1, 384, 640)
        gather(0, 1, 0, C)
        first = ((0, 0, 0), (0, 0, 1), (0, 1, 0), (0, 1, 1), (1, 0, 0), (1, 0, 1))
        for s in range(KS):
            for m, i, g in first:
                mm(m, i, g, (s,))
                if m == 0 and s == 1:
                    relu(i, g)
        gather(1, 0, 0, C)
        gather(1, 1, 0, C)
        prod(0, 0)
        mm(1, 1, 0)
        prod(0, 1)
        mm(1, 1, 1)
        turn(0)
        prod(1, 0)
        mm(0, 2, 0)
        mm(0, 2, 1)
        relu(2, 0)
        relu(2, 1)
        prod(1, 1)
        quant_h(0)
        turn(1)
        mm(1, 2, 0)
        prod(2, 0)
        mm(1, 2, 1)
        layer2(0)
        quant_h(1)
        prod(2, 1)
        mm(0, 3, 0)
        mm(0, 3, 1)
        relu(3, 0)
        relu(3, 1)
        scatter(0, 0)
        layer2(1)
        mm(1, 3, 0)
        prod(3, 0)
        turn(2)
        scatter(0, 1)
        mm(1, 3, 1)
        prod(3, 1)
        quant_h(2)
        turn(3)
        scatter(1, 0)
        layer2(2)
        scatter(1, 1)
        quant_h(3)
        scatter(2, 0)
        layer2(3)
        scatter(3, 0)
        finish(0, 0, T)
        scatter(2, 1)
        scatter(3, 1)
        finish(1, 0, T // 2)
        finish(1, T // 2, T)
